import numpy as np
import ml_dtypes


def mxq(x, axis, fmt="e4m3"):
    dtype, down = {"e4m3": (ml_dtypes.float8_e4m3fn, 7), "e5m2": (ml_dtypes.float8_e5m2, 14)}[fmt]
    v = np.moveaxis(np.asarray(x, np.float32).astype(ml_dtypes.bfloat16).astype(np.float64), axis, -1)
    blocks = v.reshape(v.shape[:-1] + (-1, 32))
    amax = np.abs(blocks).max(-1, keepdims=True)
    byte = np.maximum(np.where(amax > 0, np.frexp(amax)[1] - 1 + 127, 0) - down, 1)
    scale = np.exp2(byte - 127.0)
    codes = (blocks / scale).astype(np.float32).astype(dtype).astype(np.float64)
    return np.moveaxis((codes * scale).reshape(v.shape), -1, axis)


WIDE = False


def mx_kscale(k):
    if not WIDE:
        return np.ones(k)
    levels = np.array([10, -10, 5, -5, 0])
    if k % 512:
        return np.exp2(np.random.permutation(np.resize(levels, k // 32))).repeat(32)
    a = np.empty((k // 512, 16))
    for p in range(k // 512):
        a[p, :8] = np.random.permutation(np.resize(levels, 8))
        for g in range(8):
            far = levels[np.abs(levels - a[p, g]) >= 10]
            a[p, g + 8] = far[np.random.randint(len(far))]
    return np.exp2(a.ravel()).repeat(32)


def f64(x):
    return np.asarray(x).astype(np.float64)


def striped(idx):
    return np.tile(np.asarray(idx).reshape(-1, 16).T, (8, 1)).astype(np.uint16)


def unstriped(offs):
    return offs[:16].T.reshape(-1).astype(np.int64)


E2M1 = np.array([0.0, 0.5, 1.0, 1.5, 2.0, 3.0, 4.0, 6.0, -0.0, -0.5, -1.0, -1.5, -2.0, -3.0, -4.0, -6.0])


def pack_weight(w, fmt):
    k, n = w.shape
    w = f64(np.asarray(w, np.float32).astype(ml_dtypes.bfloat16)).reshape(k // 32, 32, n)
    amax = np.abs(w).max(1)
    if fmt == "e4m3":
        byte = np.frexp(amax)[1] - 1 + 127 - 7
    else:
        mant, ex = np.frexp(amax / 6.0)
        byte = np.where(mant > 0.5, ex, ex - 1) + 127
    byte = np.clip(np.where(amax > 0, byte, 1), 1, 254)
    scaled = (w * np.exp2(127.0 - byte)[:, None, :]).reshape(k, n).astype(np.float32)
    by_word = np.ascontiguousarray(scaled.reshape(k // 512, 128, 4, n).transpose(0, 1, 3, 2))
    if fmt == "e4m3":
        words = by_word.astype(ml_dtypes.float8_e4m3fn).view(np.uint8)
    else:
        c = by_word.astype(ml_dtypes.float4_e2m1fn).view(np.uint8) & 0xF
        words = (c[..., 0::2] | (c[..., 1::2] << 4)).reshape(k // 512, 128, 2 * n)
    return np.ascontiguousarray(words), np.ascontiguousarray(byte.astype(np.uint8).reshape(k // 512, 16, n))


def unpack_weight(words, scales, fmt):
    g, _, n = scales.shape
    words = np.ascontiguousarray(words).reshape(g, 128, n, -1)
    if fmt == "e4m3":
        vals = words.view(ml_dtypes.float8_e4m3fn).astype(np.float64)
    else:
        nib = np.empty((g, 128, n, 4), np.uint8)
        nib[..., 0::2] = words & 0xF
        nib[..., 1::2] = words >> 4
        vals = E2M1[nib]
    vals = vals * np.repeat(np.exp2(scales.astype(np.float64) - 127.0), 8, axis=1)[..., None]
    return vals.transpose(0, 1, 3, 2).reshape(g * 512, n)


D, E, T, I, G, U, Q = 512, 512, 2048, 1024, 64, 256, 128


def setup_inputs():
    n = np.random.standard_normal
    idx = np.random.permutation(T)[:I]
    idx2 = np.random.permutation(U)[:G]
    fd = mx_kscale(D)
    fe = mx_kscale(E)
    keysp = pack_weight(n((D, T)) / fd[:, None], "e2m1")
    valsp = pack_weight(n((E, T)) / fe[:, None], "e2m1")
    return {
        "query": (n((D, Q)) * 0.6 / np.sqrt(D) * fd[:, None]).astype(np.float32),
        "keys_words": keysp[0],
        "keys_scales": keysp[1],
        "pquery": (n((D, Q)) * 1.0 / np.sqrt(D) * fd[:, None]).astype(np.float32),
        "pgsum": (n((D, U)) / fd[:, None]).astype(np.float32),
        "gout": (n((E, Q)) * 1 / np.sqrt(E) * fe[:, None]).astype(np.float32),
        "vals_words": valsp[0],
        "vals_scales": valsp[1],
        "old": (0.1 * n((Q, T))).astype(np.float32),
        "offs": striped(idx),
        "offs2": striped(idx2),
    }


def reference(query, keys_words, keys_scales, pquery, pgsum, gout, vals_words, vals_scales, old, offs, offs2):
    idx = unstriped(offs)
    idx2 = unstriped(offs2)
    keysu = unpack_weight(keys_words, keys_scales, "e2m1")
    valsu = unpack_weight(vals_words, vals_scales, "e2m1")
    pqueryq = mxq(f64(pquery), 0, "e4m3")
    pgsumq = mxq(f64(pgsum), 0, "e4m3")
    b = pqueryq.T @ pgsumq
    pb = np.exp(b - np.max(b, axis=1, keepdims=True))
    mb = pb / np.sum(pb, axis=1, keepdims=True)
    queryq = mxq(f64(query), 0, "e4m3")
    keysidxg = keysu[:, idx]
    a = queryq.T @ keysidxg
    pa = np.exp(a - np.max(a, axis=1, keepdims=True))
    zi = 1.0 / pa.reshape(Q, G, I // G).sum(axis=2)
    zr = np.repeat(zi, I // G, axis=1)
    sh = pa * zr
    goutq = mxq(f64(gout), 0, "e4m3")
    valsidxg = valsu[:, idx]
    dp = goutq.T @ valsidxg
    md = (sh * dp).reshape(Q, G, I // G).sum(axis=2)
    mr = np.repeat(md, I // G, axis=1)
    mg = mb[:, idx2] * 256.0
    mgr = np.repeat(mg, I // G, axis=1)
    ds = sh * mgr * (dp - mr)
    df = np.zeros((Q, T))
    df[:, idx] = ds
    y = f64(old) + df
    return y

@@ -1,0 +1,197 @@
+from contextlib import ExitStack
+
+import concourse.mybir as mybir
+from concourse.masks import make_identity
+
+F32 = mybir.dt.float32
+BF16 = mybir.dt.bfloat16
+I32 = mybir.dt.int32
+U32 = mybir.dt.uint32
+U16 = mybir.dt.uint16
+U8 = mybir.dt.uint8
+FP8X4 = mybir.dt.float8_e4m3fn_x4
+FP4X4 = mybir.dt.float4_e2m1fn_x4
+ALU = mybir.AluOpType
+ACT = mybir.ActivationFunctionType
+AX = mybir.AxisListType
+
+P = 128
+D, T, I, G, U, Q = 512, 2048, 1024, 64, 256, 128
+PAGE = 16
+HALF = 512
+QUARTER = 256
+FLOPS = 2 * D * Q * (U + 2 * I)
+
+
+def tile_attend_gwithinpage_kernel(tc, query, keys_words, keys_scales, pquery, pgsum, gout, vals_words, vals_scales, old, offs, offs2, out):
+    nc = tc.nc
+    with ExitStack() as ctx:
+        sb = ctx.enter_context(tc.tile_pool(name="sb", bufs=1))
+        ps = ctx.enter_context(tc.psum_pool(name="ps", bufs=1))
+
+        slots = sb.tile([P, I // 16], U16, name="slots")
+        pages = sb.tile([P, G // 16], U16, name="pages")
+        kw = sb.tile([P, T], U16, name="kw", align_bytes=64)
+        vw = sb.tile([P, T], U16, name="vw", align_bytes=64)
+        ks = sb.tile([P, T], U8, name="ks", align_bytes=64)
+        vs = sb.tile([P, T], U8, name="vs", align_bytes=64)
+        df = sb.tile([P, T], F32, name="df", align_bytes=64)
+        old_sb = sb.tile([P, T], F32, name="old_sb", align_bytes=64)
+        warm = sb.tile([P, 8], F32, name="warm")
+        warm_out = sb.tile([P, 8], F32, name="warm_out")
+        ident = sb.tile([P, P], F32, name="ident", align_bytes=64)
+
+        nc.vector.memset(warm[:], 0.0)
+        nc.vector.memset(df[:], 0.0)
+        make_identity(nc, ident[:])
+
+        def load_scales(engine, plane, scales):
+            for quad in range(4):
+                engine.dma_start(out=plane[32 * quad : 32 * quad + 32, :].bitcast(I32), in_=scales[0, 4 * quad : 4 * quad + 4, :].bitcast(I32).unsqueeze(0).to_broadcast([8, 4, T // 4]))
+
+        def load_rows(src, name):
+            raw = sb.tile([P, 4, src.shape[1]], F32, name=name, tag=name, align_bytes=64)
+            nc.sync.dma_start(out=raw[:], in_=src.rearrange("(p j) w -> p j w", j=4))
+            return raw
+
+        nc.sync.dma_start(slots[:], offs)
+        nc.scalar.activation(warm_out[:], warm[:], ACT.Exp)
+        load_scales(nc.sync, ks, keys_scales)
+        nc.sync.dma_start(out=kw[:].bitcast(I32), in_=keys_words[0].bitcast(I32))
+        q_raw = load_rows(query, "q_raw")
+        g_raw = load_rows(gout, "g_raw")
+        pq_raw = load_rows(pquery, "pq_raw")
+        pg_raw = load_rows(pgsum, "pg_raw")
+        load_scales(nc.sync, vs, vals_scales)
+        nc.sync.dma_start(out=vw[:].bitcast(I32), in_=vals_words[0].bitcast(I32))
+        nc.sync.dma_start(pages[:], offs2)
+        nc.sync.dma_start(out=old_sb[:], in_=old)
+
+        def weave(dst, raw):
+            nc.scalar.copy(dst.rearrange("p (c i t) -> p c t i", i=4, t=4), raw[:].rearrange("p t (c i) -> p c t i", i=4))
+
+        q_bf = sb.tile([P, 4 * Q], BF16, name="q_bf", tag="after_q", align_bytes=64)
+        q_codes = sb.tile([P, Q], U32, name="q_codes", align_bytes=64)
+        q_scales = sb.tile([P, Q], U8, name="q_scales", align_bytes=64)
+        r_bf = sb.tile([P, 8 * Q], BF16, name="r_bf", align_bytes=64)
+        r_codes = sb.tile([P, 2 * Q], U32, name="r_codes", align_bytes=64)
+        r_scales = sb.tile([P, 2 * Q], U8, name="r_scales", align_bytes=64)
+        pg_bf = sb.tile([P, 4 * U], BF16, name="pg_bf", tag="pg_bf", align_bytes=64)
+        pg_codes = sb.tile([P, U], U32, name="pg_codes", tag="pg_codes", align_bytes=64)
+        pg_scales = sb.tile([P, U], U8, name="pg_scales", align_bytes=64)
+        weave(q_bf[:], q_raw)
+        weave(r_bf[:, 0 : 4 * Q], g_raw)
+        weave(r_bf[:, 4 * Q : 8 * Q], pq_raw)
+        weave(pg_bf[:], pg_raw)
+
+        def gather(pool_tile, dtype, lo, hi, name, tag):
+            got = sb.tile([P, hi - lo], dtype, name=name, tag=tag, align_bytes=64)
+            nc.vector.tensor_copy(got[:], pool_tile[:].indirect(slots[:, lo // 16 : hi // 16]))
+            return got
+
+        pa = sb.tile([P, I], F32, name="pa", tag="pg_raw", align_bytes=64)
+        nmax = [sb.tile([P, 1], F32, name="nmax%d" % h) for h in range(2)]
+        a_ps = [ps.tile([P, HALF], F32, name="a_ps%d" % h) for h in range(2)]
+        b_ps = ps.tile([P, U], F32, name="b_ps")
+        zt_ps = ps.tile([P, P], F32, name="zt_ps", tag="zt_ps")
+        z_ps = ps.tile([P, P], F32, name="z_ps")
+
+        def half(h):
+            return slice(h * HALF, (h + 1) * HALF)
+
+        def product(acc, codes, scales, words, word_scales):
+            nc.tensor.matmul_mx(out=acc, lhsT=codes.bitcast(FP8X4), lhsT_scale=scales, rhs=words.bitcast(FP4X4), rhs_scale=word_scales, start=True, stop=True)
+
+        def exp_half(h):
+            nc.vector.tensor_reduce(nmax[h][:], a_ps[h][:], AX.X, ALU.max, negate=True)
+            nc.scalar.activation(pa[:, half(h)], a_ps[h][:], ACT.Exp, bias=nmax[h][:])
+
+        ksg = gather(ks, U8, 0, I, "ksg", "ksg")
+        kw0 = gather(kw, U16, 0, HALF, "kw0", "kw0")
+        nc.vector.quantize_mx(out=q_codes[:].bitcast(FP8X4), scales=q_scales[:], in_=q_bf[:])
+        product(a_ps[0][:], q_codes[:], q_scales[:], kw0[:], ksg[:, half(0)])
+        kw1 = gather(kw, U16, HALF, I, "kw1", "after_q")
+        product(a_ps[1][:], q_codes[:], q_scales[:], kw1[:], ksg[:, half(1)])
+        exp_half(0)
+        exp_half(1)
+        nc.vector.quantize_mx(out=r_codes[:].bitcast(FP8X4), scales=r_scales[:], in_=r_bf[:])
+        nc.vector.quantize_mx(out=pg_codes[:].bitcast(FP8X4), scales=pg_scales[:], in_=pg_bf[:])
+        nc.tensor.matmul_mx(out=b_ps[:], lhsT=r_codes[:, Q : 2 * Q].bitcast(FP8X4), lhsT_scale=r_scales[:, Q : 2 * Q], rhs=pg_codes[:].bitcast(FP8X4), rhs_scale=pg_scales[:], start=True, stop=True)
+
+        for j in range(8):
+            nc.tensor.matmul(zt_ps[:], pa[:, j:I:8], ident[:], start=(j == 0), stop=(j == 7), is_transpose=True)
+        zt = sb.tile([P, P], F32, name="zt", tag="zt", align_bytes=64)
+        nc.scalar.activation(zt[:], zt_ps[:], ACT.Copy, scale=1.0 / 256.0)
+        nc.tensor.transpose(z_ps[:], zt[:], ident[:])
+
+        nbmax = sb.tile([P, 1], F32, name="nbmax")
+        bsum = sb.tile([P, 1], F32, name="bsum")
+        rbsum = sb.tile([P, 1], F32, name="rbsum")
+        pb = sb.tile([P, U], F32, name="pb", tag="zt", align_bytes=64)
+        mb = sb.tile([P, U], F32, name="mb")
+        zsum = sb.tile([P, G], F32, name="zsum", tag="zsum", align_bytes=64)
+        zi = sb.tile([P, G], F32, name="zi")
+        gain = sb.tile([P, G], F32, name="gain")
+        ngz = sb.tile([P, G], F32, name="ngz")
+
+        dp_ps = [ps.tile([P, HALF], F32, name="dp_ps0", tag="zt_ps"), ps.tile([P, HALF], F32, name="dp_ps1")]
+        vsg = gather(vs, U8, 0, I, "vsg", "pg_bf")
+        nc.vector.tensor_reduce(nbmax[:], b_ps[:], AX.X, ALU.max, negate=True)
+        nc.scalar.activation(pb[:], b_ps[:], ACT.Exp, bias=nbmax[:], accum_out=bsum[:])
+        vw0 = gather(vw, U16, 0, HALF, "vw0", "pg_codes")
+        product(dp_ps[0][:], r_codes[:, 0:Q], r_scales[:, 0:Q], vw0[:], vsg[:, half(0)])
+        nc.vector.reciprocal(rbsum[:], bsum[:])
+        nc.scalar.activation(mb[:], pb[:], ACT.Copy, scale=rbsum[:])
+        nc.vector.tensor_reduce(zsum[:], z_ps[:].rearrange("p (g j) -> p g j", j=2), AX.X, ALU.add)
+        vw1 = gather(vw, U16, HALF, I, "vw1", "zt")
+        product(dp_ps[1][:], r_codes[:, 0:Q], r_scales[:, 0:Q], vw1[:], vsg[:, half(1)])
+        nc.vector.reciprocal(zi[:], zsum[:])
+
+        w = [sb.tile([P, HALF], F32, name="w0", tag="zsum", align_bytes=64), sb.tile([P, HALF], F32, name="w1", align_bytes=64)]
+        wsum = [sb.tile([P, 16], F32, name="wsum%d" % c) for c in range(4)]
+        nb = [sb.tile([P, 16], F32, name="nb%d" % c) for c in range(4)]
+        centred = [sb.tile([P, QUARTER], F32, name="centred%d" % c, align_bytes=64) for c in range(4)]
+
+        def in_half(c):
+            return slice((c % 2) * QUARTER, (c % 2 + 1) * QUARTER)
+
+        def quarter(c):
+            return slice(c * QUARTER, (c + 1) * QUARTER)
+
+        def weigh(c):
+            nc.vector.tensor_tensor(w[c // 2][:, in_half(c)], dp_ps[c // 2][:, in_half(c)], pa[:, quarter(c)], ALU.mult)
+
+        def page_sum(c):
+            nc.vector.tensor_reduce(wsum[c][:], w[c // 2][:, in_half(c)].rearrange("p (g j) -> p g j", j=PAGE), AX.X, ALU.add)
+
+        def centre(c):
+            nc.vector.tensor_tensor(nb[c][:], wsum[c][:], ngz[:, 16 * c : 16 * c + 16], ALU.mult)
+            for g in range(16):
+                cols = slice(g * PAGE, (g + 1) * PAGE)
+                nc.scalar.activation(centred[c][:, cols], dp_ps[c // 2][:, in_half(c)][:, cols], ACT.Identity, bias=nb[c][:, g : g + 1], scale=gain[:, 16 * c + g : 16 * c + g + 1])
+
+        def scatter(c):
+            nc.vector.tensor_tensor(df[:].indirect(slots[:, 16 * c : 16 * c + 16]), centred[c][:], pa[:, quarter(c)], ALU.mult)
+
+        weigh(0)
+        nc.vector.tensor_tensor(gain[:], mb[:].indirect(pages[:]), zi[:], ALU.mult)
+        weigh(1)
+        nc.vector.scalar_tensor_tensor(ngz[:], gain[:], -1.0 / 256.0, zi[:], ALU.mult, ALU.mult)
+        page_sum(0)
+        page_sum(1)
+        centre(0)
+        weigh(2)
+        centre(1)
+        weigh(3)
+        page_sum(2)
+        page_sum(3)
+        centre(2)
+        centre(3)
+        for c in range(4):
+            scatter(c)
+
+        edges = [0, 256, 768, 1280, 1792, 2048]
+        for lo, hi in zip(edges[:-1], edges[1:]):
+            res = sb.tile([P, hi - lo], F32, name="res%d" % lo, align_bytes=64)
+            nc.vector.tensor_tensor(res[:], df[:, lo:hi], old_sb[:, lo:hi], ALU.add)
+            nc.sync.dma_start(out=out[:, lo:hi], in_=res[:])

@@ -43,11 +43,16 @@ def tile_attend_gwithinpage_kernel(tc, query, keys_words, keys_scales, pquery, p
 
         nc.vector.memset(warm[:], 0.0)
         nc.vector.memset(df[:], 0.0)
+        nc.gpsimd.memset(vs[:].bitcast(I32), 0)
         make_identity(nc, ident[:])
 
         def load_scales(engine, plane, scales):
             for quad in range(4):
                 engine.dma_start(out=plane[32 * quad : 32 * quad + 32, :].bitcast(I32), in_=scales[0, 4 * quad : 4 * quad + 4, :].bitcast(I32).unsqueeze(0).to_broadcast([8, 4, T // 4]))
+
+        def load_scale_rows(plane, scales):
+            for quad in range(4):
+                nc.sync.dma_start(out=plane[32 * quad : 32 * quad + 4, :].bitcast(I32), in_=scales[0, 4 * quad : 4 * quad + 4, :].bitcast(I32))
 
         def load_rows(src, name):
             raw = sb.tile([P, 4, src.shape[1]], F32, name=name, tag=name, align_bytes=64)
@@ -59,11 +64,11 @@ def tile_attend_gwithinpage_kernel(tc, query, keys_words, keys_scales, pquery, p
         load_scales(nc.sync, ks, keys_scales)
         nc.sync.dma_start(out=kw[:].bitcast(I32), in_=keys_words[0].bitcast(I32))
         q_raw = load_rows(query, "q_raw")
+        nc.sync.dma_start(out=vw[:].bitcast(I32), in_=vals_words[0].bitcast(I32))
         g_raw = load_rows(gout, "g_raw")
         pq_raw = load_rows(pquery, "pq_raw")
+        load_scale_rows(vs, vals_scales)
         pg_raw = load_rows(pgsum, "pg_raw")
-        load_scales(nc.sync, vs, vals_scales)
-        nc.sync.dma_start(out=vw[:].bitcast(I32), in_=vals_words[0].bitcast(I32))
         nc.sync.dma_start(pages[:], offs2)
         nc.sync.dma_start(out=old_sb[:], in_=old)
 
@@ -89,12 +94,13 @@ def tile_attend_gwithinpage_kernel(tc, query, keys_words, keys_scales, pquery, p
             nc.vector.tensor_copy(got[:], pool_tile[:].indirect(slots[:, lo // 16 : hi // 16]))
             return got
 
-        pa = sb.tile([P, I], F32, name="pa", tag="pg_raw", align_bytes=64)
+        pa = sb.tile([P, I], F32, name="pa", align_bytes=64)
+        dealt = sb.tile([P, 8, P], F32, name="dealt", tag="pg_raw", align_bytes=64)
         nmax = [sb.tile([P, 1], F32, name="nmax%d" % h) for h in range(2)]
         a_ps = [ps.tile([P, HALF], F32, name="a_ps%d" % h) for h in range(2)]
         b_ps = ps.tile([P, U], F32, name="b_ps")
         zt_ps = ps.tile([P, P], F32, name="zt_ps", tag="zt_ps")
-        z_ps = ps.tile([P, P], F32, name="z_ps")
+        z_ps = ps.tile([P, P], F32, name="z_ps", tag="z_ps")
 
         def half(h):
             return slice(h * HALF, (h + 1) * HALF)
@@ -104,7 +110,7 @@ def tile_attend_gwithinpage_kernel(tc, query, keys_words, keys_scales, pquery, p
 
         def exp_half(h):
             nc.vector.tensor_reduce(nmax[h][:], a_ps[h][:], AX.X, ALU.max, negate=True)
-            nc.scalar.activation(pa[:, half(h)], a_ps[h][:], ACT.Exp, bias=nmax[h][:])
+            nc.scalar.activation(dealt[:, :, 64 * h : 64 * h + 64], a_ps[h][:].rearrange("p (c j) -> p j c", j=8), ACT.Exp, bias=nmax[h][:])
 
         ksg = gather(ks, U8, 0, I, "ksg", "ksg")
         kw0 = gather(kw, U16, 0, HALF, "kw0", "kw0")
@@ -113,44 +119,45 @@ def tile_attend_gwithinpage_kernel(tc, query, keys_words, keys_scales, pquery, p
         kw1 = gather(kw, U16, HALF, I, "kw1", "after_q")
         product(a_ps[1][:], q_codes[:], q_scales[:], kw1[:], ksg[:, half(1)])
         exp_half(0)
+        vw0 = gather(vw, U16, 0, HALF, "vw0", "vw0")
         exp_half(1)
         nc.vector.quantize_mx(out=r_codes[:].bitcast(FP8X4), scales=r_scales[:], in_=r_bf[:])
         nc.vector.quantize_mx(out=pg_codes[:].bitcast(FP8X4), scales=pg_scales[:], in_=pg_bf[:])
         nc.tensor.matmul_mx(out=b_ps[:], lhsT=r_codes[:, Q : 2 * Q].bitcast(FP8X4), lhsT_scale=r_scales[:, Q : 2 * Q], rhs=pg_codes[:].bitcast(FP8X4), rhs_scale=pg_scales[:], start=True, stop=True)
 
         for j in range(8):
-            nc.tensor.matmul(zt_ps[:], pa[:, j:I:8], ident[:], start=(j == 0), stop=(j == 7), is_transpose=True)
+            nc.tensor.matmul(zt_ps[:], dealt[:, j, :], ident[:], start=(j == 0), stop=(j == 7), is_transpose=True)
         zt = sb.tile([P, P], F32, name="zt", tag="zt", align_bytes=64)
         nc.scalar.activation(zt[:], zt_ps[:], ACT.Copy, scale=1.0 / 256.0)
         nc.tensor.transpose(z_ps[:], zt[:], ident[:])
+        for h in range(2):
+            nc.scalar.activation(pa[:, half(h)], a_ps[h][:], ACT.Exp, bias=nmax[h][:])
 
-        nbmax = sb.tile([P, 1], F32, name="nbmax")
+        nbmax = sb.tile([P, 1], F32, name="nbmax", tag="nbmax", align_bytes=64)
         bsum = sb.tile([P, 1], F32, name="bsum")
         rbsum = sb.tile([P, 1], F32, name="rbsum")
-        pb = sb.tile([P, U], F32, name="pb", tag="zt", align_bytes=64)
+        pb = sb.tile([P, U], F32, name="pb")
         mb = sb.tile([P, U], F32, name="mb")
-        zsum = sb.tile([P, G], F32, name="zsum", tag="zsum", align_bytes=64)
+        zsum = sb.tile([P, G], F32, name="zsum")
         zi = sb.tile([P, G], F32, name="zi")
         gain = sb.tile([P, G], F32, name="gain")
         ngz = sb.tile([P, G], F32, name="ngz")
 
+        vs0 = gather(vs, U8, 0, HALF, "vs0", "pg_bf")
         dp_ps = [ps.tile([P, HALF], F32, name="dp_ps0", tag="zt_ps"), ps.tile([P, HALF], F32, name="dp_ps1")]
-        vsg = gather(vs, U8, 0, I, "vsg", "pg_bf")
+        product(dp_ps[0][:], r_codes[:, 0:Q], r_scales[:, 0:Q], vw0[:], vs0[:])
         nc.vector.tensor_reduce(nbmax[:], b_ps[:], AX.X, ALU.max, negate=True)
         nc.scalar.activation(pb[:], b_ps[:], ACT.Exp, bias=nbmax[:], accum_out=bsum[:])
-        vw0 = gather(vw, U16, 0, HALF, "vw0", "pg_codes")
-        product(dp_ps[0][:], r_codes[:, 0:Q], r_scales[:, 0:Q], vw0[:], vsg[:, half(0)])
+        vs1 = gather(vs, U8, HALF, I, "vs1", "pg_codes")
         nc.vector.reciprocal(rbsum[:], bsum[:])
         nc.scalar.activation(mb[:], pb[:], ACT.Copy, scale=rbsum[:])
         nc.vector.tensor_reduce(zsum[:], z_ps[:].rearrange("p (g j) -> p g j", j=2), AX.X, ALU.add)
-        vw1 = gather(vw, U16, HALF, I, "vw1", "zt")
-        product(dp_ps[1][:], r_codes[:, 0:Q], r_scales[:, 0:Q], vw1[:], vsg[:, half(1)])
         nc.vector.reciprocal(zi[:], zsum[:])
 
-        w = [sb.tile([P, HALF], F32, name="w0", tag="zsum", align_bytes=64), sb.tile([P, HALF], F32, name="w1", align_bytes=64)]
-        wsum = [sb.tile([P, 16], F32, name="wsum%d" % c) for c in range(4)]
+        w = [sb.tile([P, HALF], F32, name="w0", align_bytes=64)]
+        wsum = [sb.tile([P, 16], F32, name="wsum%d" % c, tag="wsum%d" % c, align_bytes=64) for c in range(4)]
         nb = [sb.tile([P, 16], F32, name="nb%d" % c) for c in range(4)]
-        centred = [sb.tile([P, QUARTER], F32, name="centred%d" % c, align_bytes=64) for c in range(4)]
+        centred = [sb.tile([P, QUARTER], F32, name="centred%d" % c, tag="centred%d" % c, align_bytes=64) for c in range(4)]
 
         def in_half(c):
             return slice((c % 2) * QUARTER, (c % 2 + 1) * QUARTER)
@@ -180,14 +187,18 @@ def tile_attend_gwithinpage_kernel(tc, query, keys_words, keys_scales, pquery, p
         page_sum(0)
         page_sum(1)
         centre(0)
-        weigh(2)
         centre(1)
+        vw1 = gather(vw, U16, HALF, I, "vw1", "wsum1")
+        product(dp_ps[1][:], r_codes[:, 0:Q], r_scales[:, 0:Q], vw1[:], vs1[:])
+        scatter(0)
+        w.append(sb.tile([P, HALF], F32, name="w1", tag="centred0", align_bytes=64))
+        weigh(2)
         weigh(3)
         page_sum(2)
         page_sum(3)
         centre(2)
         centre(3)
-        for c in range(4):
+        for c in range(1, 4):
             scatter(c)
 
         edges = [0, 256, 768, 1280, 1792, 2048]

@@ -37,11 +37,8 @@ def tile_attend_gwithinpage_kernel(tc, query, keys_words, keys_scales, pquery, p
         vs = sb.tile([P, T], U8, name="vs", align_bytes=64)
         df = sb.tile([P, T], F32, name="df", align_bytes=64)
         old_sb = sb.tile([P, T], F32, name="old_sb", align_bytes=64)
-        warm = sb.tile([P, 8], F32, name="warm")
-        warm_out = sb.tile([P, 8], F32, name="warm_out")
         ident = sb.tile([P, P], F32, name="ident", align_bytes=64)
 
-        nc.vector.memset(warm[:], 0.0)
         nc.vector.memset(df[:], 0.0)
         nc.gpsimd.memset(vs[:].bitcast(I32), 0)
         make_identity(nc, ident[:])
@@ -60,7 +57,6 @@ def tile_attend_gwithinpage_kernel(tc, query, keys_words, keys_scales, pquery, p
             return raw
 
         nc.sync.dma_start(slots[:], offs)
-        nc.scalar.activation(warm_out[:], warm[:], ACT.Exp)
         load_scales(nc.sync, ks, keys_scales)
         nc.sync.dma_start(out=kw[:].bitcast(I32), in_=keys_words[0].bitcast(I32))
         q_raw = load_rows(query, "q_raw")
@@ -73,7 +69,7 @@ def tile_attend_gwithinpage_kernel(tc, query, keys_words, keys_scales, pquery, p
         nc.sync.dma_start(out=old_sb[:], in_=old)
 
         def weave(dst, raw):
-            nc.scalar.copy(dst.rearrange("p (c i t) -> p c t i", i=4, t=4), raw[:].rearrange("p t (c i) -> p c t i", i=4))
+            nc.scalar.activation(dst.rearrange("p (c i t) -> p c t i", i=4, t=4), raw[:].rearrange("p t (c i) -> p c t i", i=4), ACT.Copy)
 
         q_bf = sb.tile([P, 4 * Q], BF16, name="q_bf", tag="after_q", align_bytes=64)
         q_codes = sb.tile([P, Q], U32, name="q_codes", align_bytes=64)
@@ -113,13 +109,13 @@ def tile_attend_gwithinpage_kernel(tc, query, keys_words, keys_scales, pquery, p
             nc.scalar.activation(dealt[:, :, 64 * h : 64 * h + 64], a_ps[h][:].rearrange("p (c j) -> p j c", j=8), ACT.Exp, bias=nmax[h][:])
 
         ksg = gather(ks, U8, 0, I, "ksg", "ksg")
-        kw0 = gather(kw, U16, 0, HALF, "kw0", "kw0")
+        kw0 = gather(kw, U16, 0, HALF, "kw0", "words0")
         nc.vector.quantize_mx(out=q_codes[:].bitcast(FP8X4), scales=q_scales[:], in_=q_bf[:])
         product(a_ps[0][:], q_codes[:], q_scales[:], kw0[:], ksg[:, half(0)])
         kw1 = gather(kw, U16, HALF, I, "kw1", "after_q")
         product(a_ps[1][:], q_codes[:], q_scales[:], kw1[:], ksg[:, half(1)])
         exp_half(0)
-        vw0 = gather(vw, U16, 0, HALF, "vw0", "vw0")
+        vw0 = gather(vw, U16, 0, HALF, "vw0", "words0")
         exp_half(1)
         nc.vector.quantize_mx(out=r_codes[:].bitcast(FP8X4), scales=r_scales[:], in_=r_bf[:])
         nc.vector.quantize_mx(out=pg_codes[:].bitcast(FP8X4), scales=pg_scales[:], in_=pg_bf[:])
@@ -129,6 +125,9 @@ def tile_attend_gwithinpage_kernel(tc, query, keys_words, keys_scales, pquery, p
             nc.tensor.matmul(zt_ps[:], dealt[:, j, :], ident[:], start=(j == 0), stop=(j == 7), is_transpose=True)
         zt = sb.tile([P, P], F32, name="zt", tag="zt", align_bytes=64)
         nc.scalar.activation(zt[:], zt_ps[:], ACT.Copy, scale=1.0 / 256.0)
+        vs0 = gather(vs, U8, 0, HALF, "vs0", "pg_bf")
+        dp_ps = [ps.tile([P, HALF], F32, name="dp_ps0", tag="zt_ps"), ps.tile([P, HALF], F32, name="dp_ps1")]
+        product(dp_ps[0][:], r_codes[:, 0:Q], r_scales[:, 0:Q], vw0[:], vs0[:])
         nc.tensor.transpose(z_ps[:], zt[:], ident[:])
         for h in range(2):
             nc.scalar.activation(pa[:, half(h)], a_ps[h][:], ACT.Exp, bias=nmax[h][:])
@@ -143,18 +142,13 @@ def tile_attend_gwithinpage_kernel(tc, query, keys_words, keys_scales, pquery, p
         gain = sb.tile([P, G], F32, name="gain")
         ngz = sb.tile([P, G], F32, name="ngz")
 
-        vs0 = gather(vs, U8, 0, HALF, "vs0", "pg_bf")
-        dp_ps = [ps.tile([P, HALF], F32, name="dp_ps0", tag="zt_ps"), ps.tile([P, HALF], F32, name="dp_ps1")]
-        product(dp_ps[0][:], r_codes[:, 0:Q], r_scales[:, 0:Q], vw0[:], vs0[:])
         nc.vector.tensor_reduce(nbmax[:], b_ps[:], AX.X, ALU.max, negate=True)
         nc.scalar.activation(pb[:], b_ps[:], ACT.Exp, bias=nbmax[:], accum_out=bsum[:])
         vs1 = gather(vs, U8, HALF, I, "vs1", "pg_codes")
         nc.vector.reciprocal(rbsum[:], bsum[:])
         nc.scalar.activation(mb[:], pb[:], ACT.Copy, scale=rbsum[:])
-        nc.vector.tensor_reduce(zsum[:], z_ps[:].rearrange("p (g j) -> p g j", j=2), AX.X, ALU.add)
-        nc.vector.reciprocal(zi[:], zsum[:])
 
-        w = [sb.tile([P, HALF], F32, name="w0", align_bytes=64)]
+        w = [sb.tile([P, HALF], F32, name="w0", tag="nbmax", align_bytes=64)]
         wsum = [sb.tile([P, 16], F32, name="wsum%d" % c, tag="wsum%d" % c, align_bytes=64) for c in range(4)]
         nb = [sb.tile([P, 16], F32, name="nb%d" % c) for c in range(4)]
         centred = [sb.tile([P, QUARTER], F32, name="centred%d" % c, tag="centred%d" % c, align_bytes=64) for c in range(4)]
@@ -180,15 +174,17 @@ def tile_attend_gwithinpage_kernel(tc, query, keys_words, keys_scales, pquery, p
         def scatter(c):
             nc.vector.tensor_tensor(df[:].indirect(slots[:, 16 * c : 16 * c + 16]), centred[c][:], pa[:, quarter(c)], ALU.mult)
 
+        nc.vector.tensor_reduce(zsum[:], z_ps[:].rearrange("p (g j) -> p g j", j=2), AX.X, ALU.add)
         weigh(0)
-        nc.vector.tensor_tensor(gain[:], mb[:].indirect(pages[:]), zi[:], ALU.mult)
+        nc.vector.reciprocal(zi[:], zsum[:])
         weigh(1)
-        nc.vector.scalar_tensor_tensor(ngz[:], gain[:], -1.0 / 256.0, zi[:], ALU.mult, ALU.mult)
+        nc.vector.tensor_tensor(gain[:], mb[:].indirect(pages[:]), zi[:], ALU.mult)
         page_sum(0)
+        nc.vector.scalar_tensor_tensor(ngz[:], gain[:], -1.0 / 256.0, zi[:], ALU.mult, ALU.mult)
         page_sum(1)
         centre(0)
         centre(1)
-        vw1 = gather(vw, U16, HALF, I, "vw1", "wsum1")
+        vw1 = gather(vw, U16, HALF, I, "vw1", "wsum0")
         product(dp_ps[1][:], r_codes[:, 0:Q], r_scales[:, 0:Q], vw1[:], vs1[:])
         scatter(0)
         w.append(sb.tile([P, HALF], F32, name="w1", tag="centred0", align_bytes=64))

@@ -39,13 +39,13 @@ def tile_attend_gwithinpage_kernel(tc, query, keys_words, keys_scales, pquery, p
         old_sb = sb.tile([P, T], F32, name="old_sb", align_bytes=64)
         ident = sb.tile([P, P], F32, name="ident", align_bytes=64)
 
+        nc.vector.memset(vs[:].bitcast(I32), 0)
         nc.vector.memset(df[:], 0.0)
-        nc.gpsimd.memset(vs[:].bitcast(I32), 0)
         make_identity(nc, ident[:])
 
-        def load_scales(engine, plane, scales):
+        def load_scales(plane, scales):
             for quad in range(4):
-                engine.dma_start(out=plane[32 * quad : 32 * quad + 32, :].bitcast(I32), in_=scales[0, 4 * quad : 4 * quad + 4, :].bitcast(I32).unsqueeze(0).to_broadcast([8, 4, T // 4]))
+                (nc.scalar if quad < 2 else nc.sync).dma_start(out=plane[32 * quad : 32 * quad + 32, :].bitcast(I32), in_=scales[0, 4 * quad : 4 * quad + 4, :].bitcast(I32).unsqueeze(0).to_broadcast([8, 4, T // 4]))
 
         def load_scale_rows(plane, scales):
             for quad in range(4):
@@ -57,7 +57,7 @@ def tile_attend_gwithinpage_kernel(tc, query, keys_words, keys_scales, pquery, p
             return raw
 
         nc.sync.dma_start(slots[:], offs)
-        load_scales(nc.sync, ks, keys_scales)
+        load_scales(ks, keys_scales)
         nc.sync.dma_start(out=kw[:].bitcast(I32), in_=keys_words[0].bitcast(I32))
         q_raw = load_rows(query, "q_raw")
         nc.sync.dma_start(out=vw[:].bitcast(I32), in_=vals_words[0].bitcast(I32))
@@ -197,7 +197,7 @@ def tile_attend_gwithinpage_kernel(tc, query, keys_words, keys_scales, pquery, p
         for c in range(1, 4):
             scatter(c)
 
-        edges = [0, 256, 768, 1280, 1792, 2048]
+        edges = [0, 256, 768, 1280, 1664, 1920, 2048]
         for lo, hi in zip(edges[:-1], edges[1:]):
             res = sb.tile([P, hi - lo], F32, name="res%d" % lo, align_bytes=64)
             nc.vector.tensor_tensor(res[:], df[:, lo:hi], old_sb[:, lo:hi], ALU.add)

from contextlib import ExitStack

import concourse.mybir as mybir
from concourse.masks import make_identity

F32 = mybir.dt.float32
BF16 = mybir.dt.bfloat16
I32 = mybir.dt.int32
U32 = mybir.dt.uint32
U16 = mybir.dt.uint16
U8 = mybir.dt.uint8
FP8X4 = mybir.dt.float8_e4m3fn_x4
FP4X4 = mybir.dt.float4_e2m1fn_x4
ALU = mybir.AluOpType
ACT = mybir.ActivationFunctionType
AX = mybir.AxisListType

P = 128
D, T, I, G, U, Q = 512, 2048, 1024, 64, 256, 128
PAGE = 16
HALF = 512
QUARTER = 256
FLOPS = 2 * D * Q * (U + 2 * I)


def tile_attend_gwithinpage_kernel(tc, query, keys_words, keys_scales, pquery, pgsum, gout, vals_words, vals_scales, old, offs, offs2, out):
    nc = tc.nc
    with ExitStack() as ctx:
        sb = ctx.enter_context(tc.tile_pool(name="sb", bufs=1))
        ps = ctx.enter_context(tc.psum_pool(name="ps", bufs=1))

        slots = sb.tile([P, I // 16], U16, name="slots")
        pages = sb.tile([P, G // 16], U16, name="pages")
        kw = sb.tile([P, T], U16, name="kw", align_bytes=64)
        vw = sb.tile([P, T], U16, name="vw", align_bytes=64)
        ks = sb.tile([P, T], U8, name="ks", align_bytes=64)
        vs = sb.tile([P, T], U8, name="vs", align_bytes=64)
        df = sb.tile([P, T], F32, name="df", align_bytes=64)
        old_sb = sb.tile([P, T], F32, name="old_sb", align_bytes=64)
        ident = sb.tile([P, P], F32, name="ident", align_bytes=64)

        nc.vector.memset(vs[:].bitcast(I32), 0)
        nc.vector.memset(df[:], 0.0)
        make_identity(nc, ident[:])

        def load_scales(plane, scales):
            for quad in range(4):
                (nc.scalar if quad < 2 else nc.sync).dma_start(out=plane[32 * quad : 32 * quad + 32, :].bitcast(I32), in_=scales[0, 4 * quad : 4 * quad + 4, :].bitcast(I32).unsqueeze(0).to_broadcast([8, 4, T // 4]))

        def load_scale_rows(plane, scales):
            for quad in range(4):
                nc.sync.dma_start(out=plane[32 * quad : 32 * quad + 4, :].bitcast(I32), in_=scales[0, 4 * quad : 4 * quad + 4, :].bitcast(I32))

        def load_rows(src, name):
            raw = sb.tile([P, 4, src.shape[1]], F32, name=name, tag=name, align_bytes=64)
            nc.sync.dma_start(out=raw[:], in_=src.rearrange("(p j) w -> p j w", j=4))
            return raw

        nc.sync.dma_start(slots[:], offs)
        load_scales(ks, keys_scales)
        nc.sync.dma_start(out=kw[:].bitcast(I32), in_=keys_words[0].bitcast(I32))
        q_raw = load_rows(query, "q_raw")
        nc.sync.dma_start(out=vw[:].bitcast(I32), in_=vals_words[0].bitcast(I32))
        g_raw = load_rows(gout, "g_raw")
        pq_raw = load_rows(pquery, "pq_raw")
        load_scale_rows(vs, vals_scales)
        pg_raw = load_rows(pgsum, "pg_raw")
        nc.sync.dma_start(pages[:], offs2)
        nc.sync.dma_start(out=old_sb[:], in_=old)

        def weave(dst, raw):
            nc.scalar.activation(dst.rearrange("p (c i t) -> p c t i", i=4, t=4), raw[:].rearrange("p t (c i) -> p c t i", i=4), ACT.Copy)

        q_bf = sb.tile([P, 4 * Q], BF16, name="q_bf", tag="after_q", align_bytes=64)
        q_codes = sb.tile([P, Q], U32, name="q_codes", align_bytes=64)
        q_scales = sb.tile([P, Q], U8, name="q_scales", align_bytes=64)
        r_bf = sb.tile([P, 8 * Q], BF16, name="r_bf", align_bytes=64)
        r_codes = sb.tile([P, 2 * Q], U32, name="r_codes", align_bytes=64)
        r_scales = sb.tile([P, 2 * Q], U8, name="r_scales", align_bytes=64)
        pg_bf = sb.tile([P, 4 * U], BF16, name="pg_bf", tag="pg_bf", align_bytes=64)
        pg_codes = sb.tile([P, U], U32, name="pg_codes", tag="pg_codes", align_bytes=64)
        pg_scales = sb.tile([P, U], U8, name="pg_scales", align_bytes=64)
        weave(q_bf[:], q_raw)
        weave(r_bf[:, 0 : 4 * Q], g_raw)
        weave(r_bf[:, 4 * Q : 8 * Q], pq_raw)
        weave(pg_bf[:], pg_raw)

        def gather(pool_tile, dtype, lo, hi, name, tag):
            got = sb.tile([P, hi - lo], dtype, name=name, tag=tag, align_bytes=64)
            nc.vector.tensor_copy(got[:], pool_tile[:].indirect(slots[:, lo // 16 : hi // 16]))
            return got

        pa = sb.tile([P, I], F32, name="pa", align_bytes=64)
        dealt = sb.tile([P, 8, P], F32, name="dealt", tag="pg_raw", align_bytes=64)
        nmax = [sb.tile([P, 1], F32, name="nmax%d" % h) for h in range(2)]
        a_ps = [ps.tile([P, HALF], F32, name="a_ps%d" % h) for h in range(2)]
        b_ps = ps.tile([P, U], F32, name="b_ps")
        zt_ps = ps.tile([P, P], F32, name="zt_ps", tag="zt_ps")
        z_ps = ps.tile([P, P], F32, name="z_ps", tag="z_ps")

        def half(h):
            return slice(h * HALF, (h + 1) * HALF)

        def product(acc, codes, scales, words, word_scales):
            nc.tensor.matmul_mx(out=acc, lhsT=codes.bitcast(FP8X4), lhsT_scale=scales, rhs=words.bitcast(FP4X4), rhs_scale=word_scales, start=True, stop=True)

        def exp_half(h):
            nc.vector.tensor_reduce(nmax[h][:], a_ps[h][:], AX.X, ALU.max, negate=True)
            nc.scalar.activation(dealt[:, :, 64 * h : 64 * h + 64], a_ps[h][:].rearrange("p (c j) -> p j c", j=8), ACT.Exp, bias=nmax[h][:])

        ksg = gather(ks, U8, 0, I, "ksg", "ksg")
        kw0 = gather(kw, U16, 0, HALF, "kw0", "words0")
        nc.vector.quantize_mx(out=q_codes[:].bitcast(FP8X4), scales=q_scales[:], in_=q_bf[:])
        product(a_ps[0][:], q_codes[:], q_scales[:], kw0[:], ksg[:, half(0)])
        kw1 = gather(kw, U16, HALF, I, "kw1", "after_q")
        product(a_ps[1][:], q_codes[:], q_scales[:], kw1[:], ksg[:, half(1)])
        exp_half(0)
        vw0 = gather(vw, U16, 0, HALF, "vw0", "words0")
        exp_half(1)
        nc.vector.quantize_mx(out=r_codes[:].bitcast(FP8X4), scales=r_scales[:], in_=r_bf[:])
        nc.vector.quantize_mx(out=pg_codes[:].bitcast(FP8X4), scales=pg_scales[:], in_=pg_bf[:])
        nc.tensor.matmul_mx(out=b_ps[:], lhsT=r_codes[:, Q : 2 * Q].bitcast(FP8X4), lhsT_scale=r_scales[:, Q : 2 * Q], rhs=pg_codes[:].bitcast(FP8X4), rhs_scale=pg_scales[:], start=True, stop=True)

        for j in range(8):
            nc.tensor.matmul(zt_ps[:], dealt[:, j, :], ident[:], start=(j == 0), stop=(j == 7), is_transpose=True)
        zt = sb.tile([P, P], F32, name="zt", tag="zt", align_bytes=64)
        nc.scalar.activation(zt[:], zt_ps[:], ACT.Copy, scale=1.0 / 256.0)
        vs0 = gather(vs, U8, 0, HALF, "vs0", "pg_bf")
        dp_ps = [ps.tile([P, HALF], F32, name="dp_ps0", tag="zt_ps"), ps.tile([P, HALF], F32, name="dp_ps1")]
        product(dp_ps[0][:], r_codes[:, 0:Q], r_scales[:, 0:Q], vw0[:], vs0[:])
        nc.tensor.transpose(z_ps[:], zt[:], ident[:])
        for h in range(2):
            nc.scalar.activation(pa[:, half(h)], a_ps[h][:], ACT.Exp, bias=nmax[h][:])

        nbmax = sb.tile([P, 1], F32, name="nbmax", tag="nbmax", align_bytes=64)
        bsum = sb.tile([P, 1], F32, name="bsum")
        rbsum = sb.tile([P, 1], F32, name="rbsum")
        pb = sb.tile([P, U], F32, name="pb")
        mb = sb.tile([P, U], F32, name="mb")
        zsum = sb.tile([P, G], F32, name="zsum")
        zi = sb.tile([P, G], F32, name="zi")
        gain = sb.tile([P, G], F32, name="gain")
        ngz = sb.tile([P, G], F32, name="ngz")

        nc.vector.tensor_reduce(nbmax[:], b_ps[:], AX.X, ALU.max, negate=True)
        nc.scalar.activation(pb[:], b_ps[:], ACT.Exp, bias=nbmax[:], accum_out=bsum[:])
        vs1 = gather(vs, U8, HALF, I, "vs1", "pg_codes")
        nc.vector.reciprocal(rbsum[:], bsum[:])
        nc.scalar.activation(mb[:], pb[:], ACT.Copy, scale=rbsum[:])

        w = [sb.tile([P, HALF], F32, name="w0", tag="nbmax", align_bytes=64)]
        wsum = [sb.tile([P, 16], F32, name="wsum%d" % c, tag="wsum%d" % c, align_bytes=64) for c in range(4)]
        nb = [sb.tile([P, 16], F32, name="nb%d" % c) for c in range(4)]
        centred = [sb.tile([P, QUARTER], F32, name="centred%d" % c, tag="centred%d" % c, align_bytes=64) for c in range(4)]

        def in_half(c):
            return slice((c % 2) * QUARTER, (c % 2 + 1) * QUARTER)

        def quarter(c):
            return slice(c * QUARTER, (c + 1) * QUARTER)

        def weigh(c):
            nc.vector.tensor_tensor(w[c // 2][:, in_half(c)], dp_ps[c // 2][:, in_half(c)], pa[:, quarter(c)], ALU.mult)

        def page_sum(c):
            nc.vector.tensor_reduce(wsum[c][:], w[c // 2][:, in_half(c)].rearrange("p (g j) -> p g j", j=PAGE), AX.X, ALU.add)

        def centre(c):
            nc.vector.tensor_tensor(nb[c][:], wsum[c][:], ngz[:, 16 * c : 16 * c + 16], ALU.mult)
            for g in range(16):
                cols = slice(g * PAGE, (g + 1) * PAGE)
                nc.scalar.activation(centred[c][:, cols], dp_ps[c // 2][:, in_half(c)][:, cols], ACT.Identity, bias=nb[c][:, g : g + 1], scale=gain[:, 16 * c + g : 16 * c + g + 1])

        def scatter(c):
            nc.vector.tensor_tensor(df[:].indirect(slots[:, 16 * c : 16 * c + 16]), centred[c][:], pa[:, quarter(c)], ALU.mult)

        nc.vector.tensor_reduce(zsum[:], z_ps[:].rearrange("p (g j) -> p g j", j=2), AX.X, ALU.add)
        weigh(0)
        nc.vector.reciprocal(zi[:], zsum[:])
        weigh(1)
        nc.vector.tensor_tensor(gain[:], mb[:].indirect(pages[:]), zi[:], ALU.mult)
        page_sum(0)
        nc.vector.scalar_tensor_tensor(ngz[:], gain[:], -1.0 / 256.0, zi[:], ALU.mult, ALU.mult)
        page_sum(1)
        centre(0)
        centre(1)
        vw1 = gather(vw, U16, HALF, I, "vw1", "wsum0")
        product(dp_ps[1][:], r_codes[:, 0:Q], r_scales[:, 0:Q], vw1[:], vs1[:])
        scatter(0)
        w.append(sb.tile([P, HALF], F32, name="w1", tag="centred0", align_bytes=64))
        weigh(2)
        weigh(3)
        page_sum(2)
        page_sum(3)
        centre(2)
        centre(3)
        for c in range(1, 4):
            scatter(c)

        edges = [0, 256, 768, 1280, 1664, 1920, 2048]
        for lo, hi in zip(edges[:-1], edges[1:]):
            res = sb.tile([P, hi - lo], F32, name="res%d" % lo, align_bytes=64)
            nc.vector.tensor_tensor(res[:], df[:, lo:hi], old_sb[:, lo:hi], ALU.add)
            nc.sync.dma_start(out=out[:, lo:hi], in_=res[:])
